import numpy as np
import ml_dtypes


def mxq(x, axis, fmt="e4m3"):
    dtype, down = {"e4m3": (ml_dtypes.float8_e4m3fn, 7), "e5m2": (ml_dtypes.float8_e5m2, 14)}[fmt]
    v = np.moveaxis(np.asarray(x, np.float32).astype(ml_dtypes.bfloat16).astype(np.float64), axis, -1)
    blocks = v.reshape(v.shape[:-1] + (-1, 32))
    amax = np.abs(blocks).max(-1, keepdims=True)
    byte = np.maximum(np.where(amax > 0, np.frexp(amax)[1] - 1 + 127, 0) - down, 1)
    scale = np.exp2(byte - 127.0)
    codes = (blocks / scale).astype(np.float32).astype(dtype).astype(np.float64)
    return np.moveaxis((codes * scale).reshape(v.shape), -1, axis)


WIDE = False


def mx_kscale(k):
    if not WIDE:
        return np.ones(k)
    levels = np.array([10, -10, 5, -5, 0])
    if k % 512:
        return np.exp2(np.random.permutation(np.resize(levels, k // 32))).repeat(32)
    a = np.empty((k // 512, 16))
    for p in range(k // 512):
        a[p, :8] = np.random.permutation(np.resize(levels, 8))
        for g in range(8):
            far = levels[np.abs(levels - a[p, g]) >= 10]
            a[p, g + 8] = far[np.random.randint(len(far))]
    return np.exp2(a.ravel()).repeat(32)


def f64(x):
    return np.asarray(x).astype(np.float64)


def striped(idx):
    return np.tile(idx.reshape(-1, 16).T, (8, 1)).astype(np.uint16)


def unstriped(offs):
    return offs[:16].T.reshape(-1).astype(np.int64)


def pack_weight(w):
    k, n = w.shape
    w = f64(np.asarray(w, np.float32).astype(ml_dtypes.bfloat16)).reshape(k // 32, 32, n)
    amax = np.abs(w).max(1)
    byte = np.clip(np.where(amax > 0, np.frexp(amax)[1] - 1 + 127 - 7, 1), 1, 254)
    scaled = (w * np.exp2(127.0 - byte)[:, None, :]).reshape(k, n).astype(np.float32)
    words = np.ascontiguousarray(scaled.reshape(k // 512, 128, 4, n).transpose(0, 1, 3, 2)).astype(ml_dtypes.float8_e4m3fn).view(np.uint8)
    return words, np.ascontiguousarray(byte.astype(np.uint8).reshape(k // 512, 16, n))


def unpack_weight(words, scales):
    g, p, n, _ = words.shape
    vals = np.ascontiguousarray(words).view(ml_dtypes.float8_e4m3fn).astype(np.float64) * np.repeat(np.exp2(scales.astype(np.float64) - 127.0), 8, axis=1)[..., None]
    return vals.transpose(0, 1, 3, 2).reshape(g * 512, n)


K, T, S, D, H, N = 512, 1024, 512, 4, 512, 256
P = 2 ** 7


def setup_inputs():
    n = np.random.standard_normal
    s = mx_kscale(K)[:, None]
    u = mx_kscale(H)
    packed_xT = pack_weight(n((K, T)) * s)
    packed_eT = pack_weight(n((K, T)) * s)
    packed_dT = pack_weight(n((K, T)) * s)
    return {
        "x_words": packed_xT[0],
        "x_scales": packed_xT[1],
        "e_words": packed_eT[0],
        "e_scales": packed_eT[1],
        "d_words": packed_dT[0],
        "d_scales": packed_dT[1],
        "w1": (n((K, H)) / np.sqrt(K) / s * u).astype(np.float32),
        "bl0": (np.tile(np.random.uniform(0.2, 0.8, S), (P, 1))).astype(np.float32),
        "w2": (n((K, H)) / np.sqrt(K) / s).astype(np.float32),
        "bl1": (np.tile(np.random.uniform(0.2, 0.8, S), (P, 1))).astype(np.float32),
        "w3": (n((K, H)) / np.sqrt(K) / s).astype(np.float32),
        "bl2": (np.tile(np.random.uniform(0.2, 0.8, S), (P, 1))).astype(np.float32),
        "w4": (n((H, N)) / np.sqrt(H) / u[:, None]).astype(np.float32),
        "offs": striped(np.random.permutation(T)[:S]),
        "plb": striped(np.random.permutation(T)[:S]),
        "plc": striped(np.random.permutation(T)[:S]),
    }


def reference(x_words, x_scales, e_words, e_scales, d_words, d_scales, w1, bl0, w2, bl1, w3, bl2, w4, offs, plb, plc):
    xq = unpack_weight(x_words, x_scales)[:, unstriped(offs)]
    y0 = ((mxq(f64(w1), 0, "e4m3").T @ xq)) * f64(bl0)[:1]
    f0 = y0.reshape(len(y0), -1, D).sum(axis=2)
    e_plb = unpack_weight(e_words, e_scales)[:, unstriped(plb)]
    y1 = ((mxq(f64(w2), 0, "e4m3").T @ e_plb)) * f64(bl1)[:1]
    f1 = y1.reshape(len(y1), -1, D).sum(axis=2)
    d_plc = unpack_weight(d_words, d_scales)[:, unstriped(plc)]
    y2 = ((mxq(f64(w3), 0, "e4m3").T @ d_plc)) * f64(bl2)[:1]
    f2 = y2.reshape(len(y2), -1, D).sum(axis=2)
    z = (f0 * f1) * f2
    return mxq(f64(w4), 0, "e4m3").T @ mxq(z, 0, "e4m3")

from contextlib import ExitStack

import concourse.mybir as mybir
from concourse.masks import make_identity

K, T, S, D, H, N = 512, 1024, 512, 4, 512, 256
P = 128
PACK = 4
V = S // D
HALF = H // 2

F32 = mybir.dt.float32
BF16 = mybir.dt.bfloat16
I32 = mybir.dt.int32
U32 = mybir.dt.uint32
U16 = mybir.dt.uint16
U8 = mybir.dt.uint8
FP8X4 = mybir.dt.float8_e4m3fn_x4
MULT = mybir.AluOpType.mult
ADD = mybir.AluOpType.add
COPY = mybir.ActivationFunctionType.Copy

FLOPS = 3 * 2 * K * H * S + 2 * H * N * V


def tile_picked_ytripl_none_p_kernel(
    tc, x_words, x_scales, e_words, e_scales, d_words, d_scales, w1, bl0, w2, bl1, w3, bl2, w4, offs, plb, plc, out
):
    nc = tc.nc
    words_in = [x_words, e_words, d_words]
    scales_in = [x_scales, e_scales, d_scales]
    lists_in = [offs, plb, plc]
    weights_in = [w1, w2, w3]
    blend_in = [bl0, bl1, bl2]

    with ExitStack() as ctx:
        keep = ctx.enter_context(tc.tile_pool(name="keep", bufs=1))
        psum = ctx.enter_context(tc.psum_pool(name="psum", bufs=1))

        def sb(name, shape, dtype, on=None):
            return keep.tile(shape, dtype, name=name, tag=on or name, align_bytes=64)

        lists = [keep.tile([P, S // 16], U16, name="list%d" % a) for a in range(3)]
        word_tab = [sb("word_tab%d" % a, [P, T], U32) for a in range(3)]
        scale_tab = [sb("scale_tab%d" % a, [P, T], U8) for a in range(3)]
        blend = [sb("blend%d" % a, [P, D], F32) for a in range(3)]
        w_raw = [[sb("w_raw%d_%d" % (a, u), [P, PACK, HALF], F32) for u in range(2)] for a in range(3)]
        w4_raw = sb("w4_raw", [P, PACK, N], F32)
        ident = sb("ident", [P, P], F32)
        w_codes = [sb("w_codes%d" % a, [P, H], U32) for a in range(3)]
        w_scales = [sb("w_scales%d" % a, [P, H], U8) for a in range(3)]
        w4_codes = sb("w4_codes", [P, N], U32)
        w4_scales = sb("w4_scales", [P, N], U8)
        words = {}
        listed = [sb("listed%d" % a, [P, S], U8) for a in range(3)]
        scales = [sb("scales%d" % a, [P, D, V], U8) for a in range(3)]
        w_bf = [[sb("w_bf%d_%d" % (a, u), [P, HALF, PACK], BF16) for u in range(2)] for a in range(3)]
        w4_bf = sb("w4_bf", [P, N, PACK], BF16)
        ys = {}
        feat = {}
        weighted = {}

        def clear(a):
            nc.gpsimd.memset(scale_tab[a][:].bitcast(I32), 0)

        def load_blend(a, q):
            q.dma_start(out=blend[a][:], in_=blend_in[a][0:1, :].rearrange("o (v d) -> (o v) d", d=D))

        def load_list(a):
            nc.sync.dma_start(lists[a][:], lists_in[a])

        def load_words(a):
            nc.sync.dma_start(out=word_tab[a][:].bitcast(I32), in_=words_in[a][0].rearrange("p n t -> p (n t)").bitcast(I32))

        def load_scales(a):
            for q in range(4):
                nc.sync.dma_start(
                    out=scale_tab[a][32 * q : 32 * q + 4, :].bitcast(I32),
                    in_=scales_in[a][0][4 * q : 4 * q + 4, :].bitcast(I32),
                )

        def load_w(a, u):
            nc.sync.dma_start(
                out=w_raw[a][u][:],
                in_=weights_in[a][:, u * HALF : (u + 1) * HALF].rearrange("(p j) c -> p j c", j=PACK),
            )

        def load_w4():
            nc.sync.dma_start(out=w4_raw[:], in_=w4.rearrange("(p j) c -> p j c", j=PACK))

        def cast_any(engine, grouped, raw):
            dst = grouped[:].rearrange("p (c i) j -> p c j i", i=4)
            src = raw[:].rearrange("p j (c i) -> p c j i", i=4)
            if engine == "S":
                nc.scalar.activation(out=dst, in_=src, func=COPY)
            elif engine == "G":
                nc.gpsimd.tensor_scalar(out=dst, in0=src, scalar1=1.0, scalar2=0.0, op0=MULT, op1=ADD)
            else:
                nc.vector.tensor_copy(out=dst, in_=src)

        def cast(engine, a, u):
            cast_any(engine, w_bf[a][u], w_raw[a][u])

        def quantize(grouped, codes, scale_bytes):
            nc.vector.quantize_mx(out=codes.bitcast(FP8X4), scales=scale_bytes, in_=grouped[:].rearrange("p c j -> p (c j)"))

        def quant(a, u):
            quantize(w_bf[a][u], w_codes[a][:, u * HALF : (u + 1) * HALF], w_scales[a][:, u * HALF : (u + 1) * HALF])

        def gather_words(a, on=None):
            words[a] = sb("words%d" % a, [P, D, V], U32, on)
            nc.vector.tensor_copy(words[a][:].rearrange("p d v -> p v d"), word_tab[a][:].indirect(lists[a][:]))

        def gather_scales(a):
            nc.vector.tensor_copy(listed[a][:], scale_tab[a][:].indirect(lists[a][:]))

        def deal_scales(a):
            nc.vector.tensor_copy(out=scales[a][:].rearrange("p d v -> p v d"), in_=listed[a][:].rearrange("p (v d) -> p v d", d=D))

        def product(a, d):
            y = psum.tile([P, H], F32, name="y%d" % ((D * a + d) % 6))
            nc.tensor.matmul_mx(
                out=y[:],
                lhsT=words[a][:, d, :].bitcast(FP8X4),
                lhsT_scale=scales[a][:, d, :],
                rhs=w_codes[a][:].bitcast(FP8X4),
                rhs_scale=w_scales[a][:],
                start=True,
                stop=True,
            )
            ys[(a, d)] = y

        def room(a, ds, on=None):
            shared = sb("weighted%d_%d" % (a, ds[0]), [P, len(ds), PACK, P], F32, on)
            for n, d in enumerate(ds):
                weighted[(a, d)] = shared[:, n]

        def weigh(engine, a, d):
            tile = weighted[(a, d)]
            src = ys[(a, d)][:].rearrange("p (m t) -> p t m", t=PACK)
            if engine == "S":
                nc.scalar.activation(out=tile, in_=src, func=COPY, scale=blend[a][:, d : d + 1])
            else:
                nc.vector.tensor_scalar(out=tile, in0=src, scalar1=blend[a][:, d : d + 1], scalar2=None, op0=MULT)

        def weigh_add(a, d, other):
            tile = weighted[(a, d)]
            src = ys[(a, d)][:].rearrange("p (m t) -> p t m", t=PACK)
            nc.vector.scalar_tensor_tensor(
                out=tile, in0=src, scalar=blend[a][:, d : d + 1], in1=weighted[(a, other)], op0=MULT, op1=ADD
            )

        def turn(a, d, first, last):
            if first:
                feat[a] = psum.tile([P, PACK, V], F32, name="feat%d" % (a % 2))
            for t in range(PACK):
                nc.tensor.matmul(
                    feat[a][:, t, :],
                    weighted[(a, d)][:, t, :],
                    ident[:],
                    start=(first and t == 0),
                    stop=(last and t == PACK - 1),
                    is_transpose=True,
                )

        def by_sample(a):
            return feat[a][:].rearrange("p t v -> p v t")

        for a in range(3):
            clear(a)
        make_identity(nc, ident[:])
        for a in range(3):
            load_blend(a, nc.gpsimd)
        load_words(0)
        load_list(0)
        load_w(0, 0)
        load_scales(0)
        load_w(0, 1)
        load_w(1, 0)
        load_list(1)
        load_scales(1)
        load_words(1)
        load_w(1, 1)
        load_list(2)
        load_scales(2)
        load_words(2)
        load_w(2, 0)
        load_w(2, 1)
        load_w4()

        gather_words(0)
        cast("S", 0, 0)
        gather_scales(0)
        cast("S", 0, 1)
        quant(0, 0)
        deal_scales(0)
        quant(0, 1)
        for d in range(D):
            product(0, d)
        cast("S", 1, 0)
        gather_scales(1)
        gather_words(1)
        deal_scales(1)
        room(0, [0, 1])
        for d in range(2):
            weigh("S", 0, d)
            turn(0, d, d == 0, False)
        cast("S", 1, 1)
        quant(1, 0)
        quant(1, 1)
        room(0, [2, 3], "w_raw1_1")
        weigh("S", 0, 2)
        weigh("S", 0, 3)
        for d in range(D):
            product(1, d)
        turn(0, 2, False, False)
        turn(0, 3, False, True)
        gather_scales(2)
        gather_words(2, "w_bf1_1")
        deal_scales(2)
        cast("S", 2, 0)
        cast("V", 2, 1)
        quant(2, 1)
        quant(2, 0)
        room(1, [0, 1, 2], "w_raw2_0")
        weigh("S", 1, 0)
        weigh("S", 1, 1)
        weigh("S", 1, 2)
        for d in range(D):
            product(2, d)
        room(1, [3], "w_bf2_0")
        weigh_add(1, 3, 2)
        turn(1, 0, True, False)
        turn(1, 1, False, False)
        f0 = sb("f0", [P, V, PACK], F32, "w_raw2_1")
        nc.scalar.activation(out=f0[:], in_=by_sample(0), func=COPY)
        turn(1, 3, False, True)
        cast_any("V", w4_bf, w4_raw)
        quantize(w4_bf, w4_codes[:], w4_scales[:])
        room(2, [0])
        room(2, [1])
        room(2, [2])
        room(2, [3])
        weigh("S", 2, 0)
        weigh("S", 2, 2)
        weigh_add(2, 1, 0)
        turn(2, 1, True, False)
        f01 = sb("f01", [P, V, PACK], F32, "w4_bf")
        nc.vector.tensor_tensor(out=f01[:], in0=by_sample(1), in1=f0[:], op=MULT)
        weigh_add(2, 3, 2)
        turn(2, 3, False, True)
        z_bf = sb("z_bf", [P, V, PACK], BF16)
        nc.vector.tensor_tensor(out=z_bf[:], in0=by_sample(2), in1=f01[:], op=MULT)

        z_codes = sb("z_codes", [P, V], U32)
        z_scales = sb("z_scales", [P, V], U8)
        quantize(z_bf, z_codes[:], z_scales[:])
        acc = psum.tile([P, N // P, V], F32, name="y0")
        for c in range(N // P):
            nc.tensor.matmul_mx(
                out=acc[:, c, :],
                lhsT=w4_codes[:, c * P : (c + 1) * P].bitcast(FP8X4),
                lhsT_scale=w4_scales[:, c * P : (c + 1) * P],
                rhs=z_codes[:].bitcast(FP8X4),
                rhs_scale=z_scales[:],
                start=True,
                stop=True,
            )
        result = sb("result", [P, N // P, V], F32)
        nc.scalar.activation(out=result[:], in_=acc[:], func=COPY)
        nc.sync.dma_start(out=out.rearrange("(c p) v -> p c v", p=P), in_=result[:])
